import numpy as np
import ml_dtypes


def mxq(x, axis, fmt="e4m3"):
    dtype, down = {"e4m3": (ml_dtypes.float8_e4m3fn, 7), "e5m2": (ml_dtypes.float8_e5m2, 14)}[fmt]
    v = np.moveaxis(np.asarray(x, np.float32).astype(ml_dtypes.bfloat16).astype(np.float64), axis, -1)
    blocks = v.reshape(v.shape[:-1] + (-1, 32))
    amax = np.abs(blocks).max(-1, keepdims=True)
    byte = np.maximum(np.where(amax > 0, np.frexp(amax)[1] - 1 + 127, 0) - down, 1)
    scale = np.exp2(byte - 127.0)
    codes = (blocks / scale).astype(np.float32).astype(dtype).astype(np.float64)
    return np.moveaxis((codes * scale).reshape(v.shape), -1, axis)


WIDE = False


def mx_kscale(k):
    if not WIDE:
        return np.ones(k)
    levels = np.array([10, -10, 5, -5, 0])
    if k % 512:
        return np.exp2(np.random.permutation(np.resize(levels, k // 32))).repeat(32)
    a = np.empty((k // 512, 16))
    for p in range(k // 512):
        a[p, :8] = np.random.permutation(np.resize(levels, 8))
        for g in range(8):
            far = levels[np.abs(levels - a[p, g]) >= 10]
            a[p, g + 8] = far[np.random.randint(len(far))]
    return np.exp2(a.ravel()).repeat(32)


def f64(x):
    return np.asarray(x).astype(np.float64)


def striped(idx):
    return np.tile(idx.reshape(-1, 16).T, (8, 1)).astype(np.uint16)


def unstriped(offs):
    return offs[:16].T.reshape(-1).astype(np.int64)


def striped8(idx):
    return np.concatenate([x.reshape(-1, 16).T for x in idx]).astype(np.uint16)


def runs(offs, k):
    lists = np.stack([offs[16 * r : 16 * r + 16].T.reshape(-1) for r in range(8)]).astype(np.int64)
    return lists[np.arange(k) % 512 // 64]


def pack_weight(w):
    k, n = w.shape
    w = f64(np.asarray(w, np.float32).astype(ml_dtypes.bfloat16)).reshape(k // 32, 32, n)
    amax = np.abs(w).max(1)
    byte = np.clip(np.where(amax > 0, np.frexp(amax)[1] - 1 + 127 - 7, 1), 1, 254)
    scaled = (w * np.exp2(127.0 - byte)[:, None, :]).reshape(k, n).astype(np.float32)
    words = np.ascontiguousarray(scaled.reshape(k // 512, 128, 4, n).transpose(0, 1, 3, 2)).astype(ml_dtypes.float8_e4m3fn).view(np.uint8)
    return words, np.ascontiguousarray(byte.astype(np.uint8).reshape(k // 512, 16, n))


def unpack_weight(words, scales):
    g, p, n, _ = words.shape
    vals = np.ascontiguousarray(words).view(ml_dtypes.float8_e4m3fn).astype(np.float64) * np.repeat(np.exp2(scales.astype(np.float64) - 127.0), 8, axis=1)[..., None]
    return vals.transpose(0, 1, 3, 2).reshape(g * 512, n)


def sigmoid(v):
    return 1.0 / (1.0 + np.exp(-np.maximum(v, -700.0)))

def planes(y):
    n, m = y.shape
    v = y.astype(np.float32).astype(ml_dtypes.bfloat16).astype(np.float64).reshape(n // 32, 32, m)
    top = np.abs(v).max(1)
    byte = np.clip(np.where(top > 0, np.frexp(top)[1] - 1 + 127 - 7, 1), 1, 254)
    codes = (v * np.exp2(127.0 - byte)[:, None, :]).reshape(n, m).astype(np.float32).astype(ml_dtypes.float8_e4m3fn).view(np.uint8)
    words = codes.reshape(n // 512, 128, 4, m).transpose(0, 1, 3, 2)
    return np.ascontiguousarray(words), np.ascontiguousarray(byte.astype(np.uint8).reshape(n // 512, 16, m))


K, T, S, N, G, H = 512, 1024, 512, 512, 2048, 512


def setup_inputs():
    n = np.random.standard_normal
    s = mx_kscale(K)[:, None]
    u = mx_kscale(S)
    packed_xT = pack_weight(n((K, T)) * s)
    packed_dT = pack_weight(n((K, G)) / s)
    packed_w1 = pack_weight(n((H, N)) / np.sqrt(H) / u[:, None])
    return {
        "x_words": packed_xT[0],
        "x_scales": packed_xT[1],
        "d_words": packed_dT[0],
        "d_scales": packed_dT[1],
        "gn": (np.random.uniform(0.5, 1.5, (H, 1)) * u[:, None]).astype(np.float32),
        "w1_words": packed_w1[0],
        "w1_scales": packed_w1[1],
        "offs": striped(np.random.permutation(T)[:S]),
        "k1": striped8(np.random.randint(0, G, (8, H))),
        "two": striped(np.random.permutation(T)[:S]),
        "k2": striped8(np.random.randint(0, G, (8, H))),
        "n1": striped(np.random.permutation(S)),
        "n2": striped(np.random.permutation(S)),
        "n3": striped8(np.stack([np.random.permutation(S) for _ in range(8)])),
    }


def reference(x_words, x_scales, d_words, d_scales, gn, w1_words, w1_scales, offs, k1, two, k2, n1, n2, n3):
    d_k1 = unpack_weight(d_words, d_scales)[np.arange(K)[:, None], runs(k1, K)]
    xq = unpack_weight(x_words, x_scales)[:, unstriped(offs)]
    a = 0.0625 * (d_k1.T @ xq)
    d_k2 = unpack_weight(d_words, d_scales)[np.arange(K)[:, None], runs(k2, K)]
    x_two = unpack_weight(x_words, x_scales)[:, unstriped(two)]
    b = 0.0625 * (d_k2.T @ x_two)
    z = f64(gn) * (a * (sigmoid(b[:, unstriped(n2)])) - (0.5 * a[:, unstriped(n1)]))
    h = unpack_weight(w1_words, w1_scales).T @ mxq(z, 0, "e4m3")
    out_0 = h / (np.abs(h[np.arange(N)[:, None], runs(n3, N)]) + 0.5)
    return (out_0,) + planes(out_0)

@@ -1,0 +1,229 @@
+from contextlib import ExitStack
+
+import concourse.mybir as mybir
+
+K, T, S, N, G, H = 512, 1024, 512, 512, 2048, 512
+FLOPS = 2 * K * H * S * 2 + 2 * H * N * S
+
+F32 = mybir.dt.float32
+BF16 = mybir.dt.bfloat16
+I32 = mybir.dt.int32
+U32 = mybir.dt.uint32
+U16 = mybir.dt.uint16
+U8 = mybir.dt.uint8
+FP8X4 = mybir.dt.float8_e4m3fn_x4
+ACT = mybir.ActivationFunctionType
+ALU = mybir.AluOpType
+
+P = 128
+PACK = 4
+LANES = 16
+Z_CHUNKS = [(0, 128), (128, 384), (384, 512)]
+OUT_CHUNKS = [(0, 256), (256, 512)]
+
+
+def tile_picked_twpqgatebnorm_none_po_kernel(
+    tc, x_words, x_scales, d_words, d_scales, gn, w1_words, w1_scales, offs, k1, two, k2, n1, n2, n3, out_0, out_1, out_2
+):
+    nc = tc.nc
+
+    with ExitStack() as ctx:
+        keep = ctx.enter_context(tc.tile_pool(name="keep", bufs=1))
+        psum = ctx.enter_context(tc.psum_pool(name="psum", bufs=1))
+
+        def load_list(name, src):
+            tile = keep.tile([P, S // LANES], U16, name=name)
+            nc.sync.dma_start(tile[:], src)
+            return tile
+
+        def entries(lst, lo, hi):
+            return lst[:, lo // LANES : hi // LANES]
+
+        def load_words(name, src, cols, queue):
+            tile = keep.tile([P, cols], I32, name=name, align_bytes=64)
+            queue.dma_start(out=tile[:], in_=src[0].rearrange("p n t -> p (n t)").bitcast(I32))
+            return tile
+
+        def load_scale_rows(name, src, cols):
+            tile = keep.tile([P, cols], U8, name=name, align_bytes=64)
+            rows = src[0].bitcast(I32)
+            nc.sync.dma_start(out=tile[:].bitcast(I32), in_=rows.unsqueeze(1).broadcast_to([16, 8, cols // 4]))
+            return tile
+
+        k2_t = load_list("k2_t", k2)
+        d_rows = load_scale_rows("d_rows", d_scales, G)
+        two_t = load_list("two_t", two)
+        x_rows = load_scale_rows("x_rows", x_scales, T)
+        x_tab = load_words("x_tab", x_words, T, nc.sync)
+        d_tab = load_words("d_tab", d_words, G, nc.sync)
+        k1_t = load_list("k1_t", k1)
+        offs_t = load_list("offs_t", offs)
+        n2_t = load_list("n2_t", n2)
+        n1_t = load_list("n1_t", n1)
+        n3_t = load_list("n3_t", n3)
+
+        gn_t = keep.tile([P, PACK], F32, name="gn_t")
+        nc.gpsimd.dma_start(out=gn_t[:], in_=gn.rearrange("(p t) o -> p (t o)", t=PACK))
+        w_raw = load_words("w_raw", w1_words, N, nc.gpsimd)
+        w_rows = keep.tile([P, N], U8, name="w_rows", align_bytes=64)
+        nc.gpsimd.memset(w_rows[:].bitcast(I32), 0)
+        for q in range(4):
+            nc.gpsimd.dma_start(
+                out=w_rows[32 * q : 32 * q + 4, :].bitcast(I32), in_=w1_scales[0, 4 * q : 4 * q + 4, :].bitcast(I32)
+            )
+        gain = keep.tile([P, PACK], F32, name="gain")
+        nc.gpsimd.tensor_scalar(gain[:], gn_t[:], -0.5 * 0.0625, 0.0, ALU.mult, ALU.add)
+
+        def deal(src):
+            return src.rearrange("p (m t) -> p t m", t=PACK)
+
+        def dealt(dst):
+            return dst.rearrange("p (t m) -> p t m", t=PACK)
+
+        def coded_product(side, codes_t, tokens_t):
+            picked = keep.tile([P, H + S], U8, name=side + "_picked", align_bytes=64)
+            placed = keep.tile([P, H + S], U8, name=side + "_placed", align_bytes=64)
+            nc.vector.memset(placed[:].bitcast(I32), 0)
+            nc.vector.tensor_copy(picked[:, :H], d_rows[:].indirect(codes_t[:]))
+            nc.vector.tensor_copy(picked[:, H:], x_rows[:].indirect(tokens_t[:]))
+            for r in range(4):
+                nc.sync.dma_start(out=placed[r:P:32, :].bitcast(I32), in_=picked[8 * r : P : 32, :].bitcast(I32))
+            x_pick = keep.tile([P, S], U32, name=side + "_x_pick", align_bytes=64)
+            nc.vector.tensor_copy(x_pick[:], x_tab[:].bitcast(U32).indirect(tokens_t[:]))
+            d_pick = keep.tile([P, H], U32, name=side + "_d_pick", align_bytes=64)
+            nc.vector.tensor_copy(d_pick[:], d_tab[:].bitcast(U32).indirect(codes_t[:]))
+            d_codes = keep.tile([P, H], U32, name=side + "_d_codes", align_bytes=64)
+            nc.vector.tensor_copy(dealt(d_codes[:]), deal(d_pick[:]))
+            d_plane = keep.tile([P, H], U8, name=side + "_d_plane", align_bytes=64)
+            nc.vector.tensor_copy(dealt(d_plane[:]), deal(placed[:, :H]))
+            banks = []
+            for t in range(PACK):
+                bank = psum.tile([P, S], F32, name=side + "_bank%d" % t, tag=side + "_bank%d" % t)
+                cols = slice(P * t, P * (t + 1))
+                nc.tensor.matmul_mx(
+                    out=bank[:],
+                    lhsT=d_codes[:, cols].bitcast(FP8X4),
+                    lhsT_scale=d_plane[:, cols],
+                    rhs=x_pick[:].bitcast(FP8X4),
+                    rhs_scale=placed[:, H:],
+                    start=True,
+                    stop=True,
+                )
+                banks.append(bank)
+            return banks
+
+        w_codes = keep.tile([P, N], U32, name="w_codes", align_bytes=64)
+        w_plane = keep.tile([P, N], U8, name="w_plane", align_bytes=64)
+
+        b_banks = coded_product("b", k2_t, two_t)
+        sig = []
+        for t in range(PACK):
+            tile = keep.tile([P, S], F32, name="sig%d" % t)
+            nc.scalar.activation(tile[:], b_banks[t][:], ACT.Sigmoid, scale=0.0625)
+            sig.append(tile)
+        gate = []
+        for t in range(PACK):
+            gate.append(keep.tile([P, S], F32, name="gate%d" % t))
+        for t in range(PACK - 1):
+            for lo in (0, 256):
+                nc.scalar.activation(gate[t][:, lo : lo + 256], sig[t][:].indirect(entries(n2_t, lo, lo + 256)), ACT.Copy)
+
+        a_banks = coded_product("a", k1_t, offs_t)
+        for lo in (0, 256):
+            nc.vector.tensor_copy(gate[3][:, lo : lo + 256], sig[3][:].indirect(entries(n2_t, lo, lo + 256)))
+        nc.vector.tensor_copy(dealt(w_plane[:]), deal(w_rows[:]))
+
+        half = []
+        for t in range(PACK):
+            tile = keep.tile([P, S], F32, name="half%d" % t)
+            nc.scalar.activation(tile[:], a_banks[t][:], ACT.Copy, scale=gain[:, t : t + 1])
+            half.append(tile)
+
+        gated = []
+        other = []
+        for c, (lo, hi) in enumerate(Z_CHUNKS):
+            gated.append(keep.tile([P, PACK, hi - lo], F32, name="gated%d" % c))
+            other.append(keep.tile([P, PACK, hi - lo], F32, name="other%d" % c))
+        for t in range(PACK):
+            for c, (lo, hi) in enumerate(Z_CHUNKS):
+                nc.vector.scalar_tensor_tensor(
+                    gated[c][:, t, :], gate[t][:, lo:hi], -2.0, half[t][:, lo:hi], ALU.mult, ALU.mult
+                )
+            lo, hi = Z_CHUNKS[0]
+            nc.vector.tensor_tensor(other[0][:, t, :], half[t][:].indirect(entries(n1_t, lo, hi)), gated[0][:, t, :], ALU.add)
+        for c in (1, 2):
+            lo, hi = Z_CHUNKS[c]
+            for t in range(PACK):
+                nc.scalar.activation(other[c][:, t, :], half[t][:].indirect(entries(n1_t, lo, hi)), ACT.Copy)
+        nc.scalar.copy(dealt(w_codes[:]), deal(w_raw[:].bitcast(U32)))
+
+        def woven(dst):
+            return dst.rearrange("p (c i) t -> p c t i", i=4)
+
+        def by_fours(src):
+            return src.rearrange("p t (c i) -> p c t i", i=4)
+
+        h_banks = []
+        for t in range(PACK):
+            h_banks.append(psum.tile([P, S], F32, name="h_bank%d" % t, tag="b_bank%d" % t))
+        for c, (lo, hi) in enumerate(Z_CHUNKS):
+            z_bf = keep.tile([P, hi - lo, PACK], BF16, name="z_bf%d" % c, align_bytes=64)
+            if c == 0:
+                nc.vector.tensor_copy(woven(z_bf[:]), by_fours(other[c][:]))
+            else:
+                nc.vector.tensor_tensor(woven(z_bf[:]), by_fours(gated[c][:]), by_fours(other[c][:]), ALU.add)
+            z_codes = keep.tile([P, hi - lo], U32, name="z_codes%d" % c, align_bytes=64)
+            z_plane = keep.tile([P, hi - lo], U8, name="z_plane%d" % c, align_bytes=64)
+            nc.vector.quantize_mx(
+                out=z_codes[:].bitcast(FP8X4), scales=z_plane[:], in_=z_bf[:].rearrange("p c t -> p (c t)")
+            )
+            for t in range(PACK):
+                cols = slice(P * t, P * (t + 1))
+                nc.tensor.matmul_mx(
+                    out=h_banks[t][:, lo:hi],
+                    lhsT=w_codes[:, cols].bitcast(FP8X4),
+                    lhsT_scale=w_plane[:, cols],
+                    rhs=z_codes[:].bitcast(FP8X4),
+                    rhs_scale=z_plane[:],
+                    start=True,
+                    stop=True,
+                )
+
+        half_bias = keep.tile([P, 1], F32, name="half_bias")
+        nc.gpsimd.memset(half_bias[:], 0.5)
+        inv = []
+        for t in range(PACK):
+            size = keep.tile([P, S], F32, name="size%d" % t)
+            nc.scalar.activation(size[:], h_banks[t][:], ACT.Abs)
+            root = keep.tile([P, S], F32, name="root%d" % t)
+            nc.scalar.activation(root[:], size[:], ACT.Abs_reciprocal_sqrt, bias=half_bias[:])
+            tile = keep.tile([P, S], F32, name="inv%d" % t)
+            nc.vector.tensor_tensor(tile[:], root[:], root[:], ALU.mult)
+            inv.append(tile)
+
+        out_rows = out_0.rearrange("(p t) j -> p t j", t=PACK)
+        out_words = out_1[0].rearrange("p n t -> p (n t)").bitcast(I32)
+        y_plane = keep.tile([P, S], U8, name="y_plane", align_bytes=64)
+        for c, (lo, hi) in enumerate(OUT_CHUNKS):
+            y = keep.tile([P, PACK, hi - lo], F32, name="y%d" % c)
+            for t in range(PACK):
+                fetched = keep.tile([P, hi - lo], F32, name="fetched%d_%d" % (c, t))
+                window = inv[t][:].indirect(entries(n3_t, lo, hi))
+                if c == 0:
+                    nc.vector.tensor_copy(fetched[:], window)
+                else:
+                    nc.scalar.activation(fetched[:], window, ACT.Copy)
+                nc.vector.tensor_tensor(y[:, t, :], h_banks[t][:, lo:hi], fetched[:], ALU.mult)
+            nc.sync.dma_start(out=out_rows[:, :, lo:hi], in_=y[:])
+            y_bf = keep.tile([P, hi - lo, PACK], BF16, name="y_bf%d" % c, align_bytes=64)
+            nc.vector.tensor_copy(woven(y_bf[:]), by_fours(y[:]))
+            y_codes = keep.tile([P, hi - lo], I32, name="y_codes%d" % c, align_bytes=64)
+            nc.vector.quantize_mx(
+                out=y_codes[:].bitcast(FP8X4), scales=y_plane[:, lo:hi], in_=y_bf[:].rearrange("p c t -> p (c t)")
+            )
+            nc.sync.dma_start(out=out_words[:, lo:hi], in_=y_codes[:])
+        for q in range(4):
+            queue = nc.sync if q % 2 == 0 else nc.scalar
+            queue.dma_start(
+                out=out_2[0, 4 * q : 4 * q + 4, :].bitcast(I32), in_=y_plane[32 * q : 32 * q + 4, :].bitcast(I32)
+            )

@@ -18,8 +18,13 @@ ALU = mybir.AluOpType
 P = 128
 PACK = 4
 LANES = 16
-Z_CHUNKS = [(0, 128), (128, 384), (384, 512)]
-OUT_CHUNKS = [(0, 256), (256, 512)]
+W = 128
+CHUNKS = S // W
+Z_ON_VECTOR = (1, 3)
+H_ON_VECTOR = ()
+ROUND_ON_SCALAR = (1, 2)
+FETCH_ON_VECTOR = (0,)
+WARM = False
 
 
 def tile_picked_twpqgatebnorm_none_po_kernel(
@@ -29,6 +34,7 @@ def tile_picked_twpqgatebnorm_none_po_kernel(
 
     with ExitStack() as ctx:
         keep = ctx.enter_context(tc.tile_pool(name="keep", bufs=1))
+        reuse = ctx.enter_context(tc.tile_pool(name="reuse", bufs=1))
         psum = ctx.enter_context(tc.psum_pool(name="psum", bufs=1))
 
         def load_list(name, src):
@@ -50,21 +56,21 @@ def tile_picked_twpqgatebnorm_none_po_kernel(
             nc.sync.dma_start(out=tile[:].bitcast(I32), in_=rows.unsqueeze(1).broadcast_to([16, 8, cols // 4]))
             return tile
 
-        k2_t = load_list("k2_t", k2)
-        d_rows = load_scale_rows("d_rows", d_scales, G)
         two_t = load_list("two_t", two)
         x_rows = load_scale_rows("x_rows", x_scales, T)
-        x_tab = load_words("x_tab", x_words, T, nc.sync)
+        k2_t = load_list("k2_t", k2)
+        d_rows = load_scale_rows("d_rows", d_scales, G)
         d_tab = load_words("d_tab", d_words, G, nc.sync)
-        k1_t = load_list("k1_t", k1)
-        offs_t = load_list("offs_t", offs)
         n2_t = load_list("n2_t", n2)
         n1_t = load_list("n1_t", n1)
         n3_t = load_list("n3_t", n3)
+        x_tab = load_words("x_tab", x_words, T, nc.sync)
+        k1_t = load_list("k1_t", k1)
+        offs_t = load_list("offs_t", offs)
+        w_raw = load_words("w_raw", w1_words, N, nc.sync)
 
         gn_t = keep.tile([P, PACK], F32, name="gn_t")
         nc.gpsimd.dma_start(out=gn_t[:], in_=gn.rearrange("(p t) o -> p (t o)", t=PACK))
-        w_raw = load_words("w_raw", w1_words, N, nc.gpsimd)
         w_rows = keep.tile([P, N], U8, name="w_rows", align_bytes=64)
         nc.gpsimd.memset(w_rows[:].bitcast(I32), 0)
         for q in range(4):
@@ -80,18 +86,20 @@ def tile_picked_twpqgatebnorm_none_po_kernel(
         def dealt(dst):
             return dst.rearrange("p (t m) -> p t m", t=PACK)
 
-        def coded_product(side, codes_t, tokens_t):
-            picked = keep.tile([P, H + S], U8, name=side + "_picked", align_bytes=64)
+        def coded_product(side, codes_t, tokens_t, picked_at, d_pick_at):
+            picked = reuse.tile([P, H + S], U8, name=side + "_picked", align_bytes=64, offset=picked_at)
             placed = keep.tile([P, H + S], U8, name=side + "_placed", align_bytes=64)
             nc.vector.memset(placed[:].bitcast(I32), 0)
-            nc.vector.tensor_copy(picked[:, :H], d_rows[:].indirect(codes_t[:]))
             nc.vector.tensor_copy(picked[:, H:], x_rows[:].indirect(tokens_t[:]))
-            for r in range(4):
-                nc.sync.dma_start(out=placed[r:P:32, :].bitcast(I32), in_=picked[8 * r : P : 32, :].bitcast(I32))
-            x_pick = keep.tile([P, S], U32, name=side + "_x_pick", align_bytes=64)
-            nc.vector.tensor_copy(x_pick[:], x_tab[:].bitcast(U32).indirect(tokens_t[:]))
-            d_pick = keep.tile([P, H], U32, name=side + "_d_pick", align_bytes=64)
+            nc.vector.tensor_copy(picked[:, :H], d_rows[:].indirect(codes_t[:]))
+            for q in range(4):
+                nc.sync.dma_start(
+                    out=placed[32 * q : 32 * q + 4, :].bitcast(I32), in_=picked[32 * q : 32 * q + 32 : 8, :].bitcast(I32)
+                )
+            d_pick = reuse.tile([P, H], U32, name=side + "_d_pick", align_bytes=64, offset=d_pick_at)
             nc.vector.tensor_copy(d_pick[:], d_tab[:].bitcast(U32).indirect(codes_t[:]))
+            x_pick = keep.tile([P, S], U32, name=side + "_x_pick", tag="x_pick", align_bytes=64)
+            nc.vector.tensor_copy(x_pick[:], x_tab[:].bitcast(U32).indirect(tokens_t[:]))
             d_codes = keep.tile([P, H], U32, name=side + "_d_codes", align_bytes=64)
             nc.vector.tensor_copy(dealt(d_codes[:]), deal(d_pick[:]))
             d_plane = keep.tile([P, H], U8, name=side + "_d_plane", align_bytes=64)
@@ -113,22 +121,23 @@ def tile_picked_twpqgatebnorm_none_po_kernel(
             return banks
 
         w_codes = keep.tile([P, N], U32, name="w_codes", align_bytes=64)
-        w_plane = keep.tile([P, N], U8, name="w_plane", align_bytes=64)
+        w_plane = reuse.tile([P, N], U8, name="w_plane", align_bytes=64, offset=4096 + 512)
 
-        b_banks = coded_product("b", k2_t, two_t)
+        b_banks = coded_product("b", k2_t, two_t, 4096, 8192)
         sig = []
         for t in range(PACK):
             tile = keep.tile([P, S], F32, name="sig%d" % t)
             nc.scalar.activation(tile[:], b_banks[t][:], ACT.Sigmoid, scale=0.0625)
             sig.append(tile)
         gate = []
-        for t in range(PACK):
+        for t in range(PACK - 1):
             gate.append(keep.tile([P, S], F32, name="gate%d" % t))
+        gate.append(reuse.tile([P, S], F32, name="gate3", align_bytes=64, offset=4096 + 512 + 768))
         for t in range(PACK - 1):
             for lo in (0, 256):
                 nc.scalar.activation(gate[t][:, lo : lo + 256], sig[t][:].indirect(entries(n2_t, lo, lo + 256)), ACT.Copy)
 
-        a_banks = coded_product("a", k1_t, offs_t)
+        a_banks = coded_product("a", k1_t, offs_t, 4096 + 512, 4096 - 2048 + 256)
         for lo in (0, 256):
             nc.vector.tensor_copy(gate[3][:, lo : lo + 256], sig[3][:].indirect(entries(n2_t, lo, lo + 256)))
         nc.vector.tensor_copy(dealt(w_plane[:]), deal(w_rows[:]))
@@ -139,22 +148,6 @@ def tile_picked_twpqgatebnorm_none_po_kernel(
             nc.scalar.activation(tile[:], a_banks[t][:], ACT.Copy, scale=gain[:, t : t + 1])
             half.append(tile)
 
-        gated = []
-        other = []
-        for c, (lo, hi) in enumerate(Z_CHUNKS):
-            gated.append(keep.tile([P, PACK, hi - lo], F32, name="gated%d" % c))
-            other.append(keep.tile([P, PACK, hi - lo], F32, name="other%d" % c))
-        for t in range(PACK):
-            for c, (lo, hi) in enumerate(Z_CHUNKS):
-                nc.vector.scalar_tensor_tensor(
-                    gated[c][:, t, :], gate[t][:, lo:hi], -2.0, half[t][:, lo:hi], ALU.mult, ALU.mult
-                )
-            lo, hi = Z_CHUNKS[0]
-            nc.vector.tensor_tensor(other[0][:, t, :], half[t][:].indirect(entries(n1_t, lo, hi)), gated[0][:, t, :], ALU.add)
-        for c in (1, 2):
-            lo, hi = Z_CHUNKS[c]
-            for t in range(PACK):
-                nc.scalar.activation(other[c][:, t, :], half[t][:].indirect(entries(n1_t, lo, hi)), ACT.Copy)
         nc.scalar.copy(dealt(w_codes[:]), deal(w_raw[:].bitcast(U32)))
 
         def woven(dst):
@@ -163,24 +156,40 @@ def tile_picked_twpqgatebnorm_none_po_kernel(
         def by_fours(src):
             return src.rearrange("p t (c i) -> p c t i", i=4)
 
-        h_banks = []
+        gated = keep.tile([P, PACK, S], F32, name="gated")
         for t in range(PACK):
-            h_banks.append(psum.tile([P, S], F32, name="h_bank%d" % t, tag="b_bank%d" % t))
-        for c, (lo, hi) in enumerate(Z_CHUNKS):
-            z_bf = keep.tile([P, hi - lo, PACK], BF16, name="z_bf%d" % c, align_bytes=64)
-            if c == 0:
-                nc.vector.tensor_copy(woven(z_bf[:]), by_fours(other[c][:]))
+            nc.vector.scalar_tensor_tensor(gated[:, t, :], gate[t][:], -2.0, half[t][:], ALU.mult, ALU.mult)
+
+        half_bias = keep.tile([P, 1], F32, name="half_bias")
+        nc.gpsimd.memset(half_bias[:], 0.5)
+        inv = []
+        for t in range(PACK):
+            inv.append(keep.tile([P, S], F32, name="inv%d" % t))
+
+        h_src = []
+        for c in range(CHUNKS):
+            lo, hi = W * c, W * (c + 1)
+            other = keep.tile([P, PACK, W], F32, name="other%d" % c)
+            z_bf = keep.tile([P, W, PACK], BF16, name="z_bf%d" % c, align_bytes=64)
+            if c in Z_ON_VECTOR:
+                for t in range(PACK):
+                    nc.vector.tensor_tensor(other[:, t, :], half[t][:].indirect(entries(n1_t, lo, hi)), gated[:, t, lo:hi], ALU.add)
+                nc.vector.tensor_copy(woven(z_bf[:]), by_fours(other[:]))
             else:
-                nc.vector.tensor_tensor(woven(z_bf[:]), by_fours(gated[c][:]), by_fours(other[c][:]), ALU.add)
-            z_codes = keep.tile([P, hi - lo], U32, name="z_codes%d" % c, align_bytes=64)
-            z_plane = keep.tile([P, hi - lo], U8, name="z_plane%d" % c, align_bytes=64)
+                for t in range(PACK):
+                    nc.scalar.activation(other[:, t, :], half[t][:].indirect(entries(n1_t, lo, hi)), ACT.Copy)
+                last_other = other
+                nc.vector.tensor_tensor(woven(z_bf[:]), by_fours(gated[:, :, lo:hi]), by_fours(other[:]), ALU.add)
+            z_codes = keep.tile([P, W], U32, name="z_codes%d" % c, align_bytes=64)
+            z_plane = keep.tile([P, W], U8, name="z_plane%d" % c, align_bytes=64)
             nc.vector.quantize_mx(
                 out=z_codes[:].bitcast(FP8X4), scales=z_plane[:], in_=z_bf[:].rearrange("p c t -> p (c t)")
             )
+            bank = psum.tile([P, PACK, W], F32, name="h_bank%d" % c, tag="b_bank%d" % c)
             for t in range(PACK):
                 cols = slice(P * t, P * (t + 1))
                 nc.tensor.matmul_mx(
-                    out=h_banks[t][:, lo:hi],
+                    out=bank[:, t, :],
                     lhsT=w_codes[:, cols].bitcast(FP8X4),
                     lhsT_scale=w_plane[:, cols],
                     rhs=z_codes[:].bitcast(FP8X4),
@@ -188,36 +197,50 @@ def tile_picked_twpqgatebnorm_none_po_kernel(
                     start=True,
                     stop=True,
                 )
+            h_src.append(bank)
 
-        half_bias = keep.tile([P, 1], F32, name="half_bias")
-        nc.gpsimd.memset(half_bias[:], 0.5)
-        inv = []
-        for t in range(PACK):
-            size = keep.tile([P, S], F32, name="size%d" % t)
-            nc.scalar.activation(size[:], h_banks[t][:], ACT.Abs)
-            root = keep.tile([P, S], F32, name="root%d" % t)
+        if WARM:
+            warm = keep.tile([P, 1], F32, name="warm")
+            nc.scalar.activation(warm[:], last_other[:, 3, 0:1], ACT.Abs_reciprocal_sqrt, bias=half_bias[:])
+        for c in range(CHUNKS):
+            lo, hi = W * c, W * (c + 1)
+            size = keep.tile([P, PACK, W], F32, name="size%d" % c)
+            if c in H_ON_VECTOR:
+                h_sb = keep.tile([P, PACK, W], F32, name="h_sb%d" % c)
+                nc.vector.tensor_copy(h_sb[:], h_src[c][:])
+                nc.vector.scalar_tensor_tensor(size[:], h_sb[:], -1.0, h_sb[:], ALU.mult, ALU.max)
+                h_src[c] = h_sb
+            else:
+                nc.scalar.activation(size[:], h_src[c][:], ACT.Abs)
+            root = keep.tile([P, PACK, W], F32, name="root%d" % c)
             nc.scalar.activation(root[:], size[:], ACT.Abs_reciprocal_sqrt, bias=half_bias[:])
-            tile = keep.tile([P, S], F32, name="inv%d" % t)
-            nc.vector.tensor_tensor(tile[:], root[:], root[:], ALU.mult)
-            inv.append(tile)
+            for t in range(PACK):
+                nc.vector.tensor_tensor(inv[t][:, lo:hi], root[:, t, :], root[:, t, :], ALU.mult)
 
         out_rows = out_0.rearrange("(p t) j -> p t j", t=PACK)
         out_words = out_1[0].rearrange("p n t -> p (n t)").bitcast(I32)
         y_plane = keep.tile([P, S], U8, name="y_plane", align_bytes=64)
-        for c, (lo, hi) in enumerate(OUT_CHUNKS):
-            y = keep.tile([P, PACK, hi - lo], F32, name="y%d" % c)
-            for t in range(PACK):
-                fetched = keep.tile([P, hi - lo], F32, name="fetched%d_%d" % (c, t))
-                window = inv[t][:].indirect(entries(n3_t, lo, hi))
-                if c == 0:
-                    nc.vector.tensor_copy(fetched[:], window)
-                else:
-                    nc.scalar.activation(fetched[:], window, ACT.Copy)
-                nc.vector.tensor_tensor(y[:, t, :], h_banks[t][:, lo:hi], fetched[:], ALU.mult)
+        for c in range(CHUNKS):
+            lo, hi = W * c, W * (c + 1)
+            y = keep.tile([P, PACK, W], F32, name="y%d" % c)
+            if c in H_ON_VECTOR:
+                for t in range(PACK):
+                    nc.vector.tensor_tensor(y[:, t, :], inv[t][:].indirect(entries(n3_t, lo, hi)), h_src[c][:, t, :], ALU.mult)
+            else:
+                fetched = keep.tile([P, PACK, W], F32, name="fetched%d" % c)
+                for t in range(PACK):
+                    if c in FETCH_ON_VECTOR:
+                        nc.vector.tensor_copy(fetched[:, t, :], inv[t][:].indirect(entries(n3_t, lo, hi)))
+                    else:
+                        nc.scalar.activation(fetched[:, t, :], inv[t][:].indirect(entries(n3_t, lo, hi)), ACT.Copy)
+                nc.vector.tensor_tensor(y[:], h_src[c][:], fetched[:], ALU.mult)
             nc.sync.dma_start(out=out_rows[:, :, lo:hi], in_=y[:])
-            y_bf = keep.tile([P, hi - lo, PACK], BF16, name="y_bf%d" % c, align_bytes=64)
-            nc.vector.tensor_copy(woven(y_bf[:]), by_fours(y[:]))
-            y_codes = keep.tile([P, hi - lo], I32, name="y_codes%d" % c, align_bytes=64)
+            y_bf = keep.tile([P, W, PACK], BF16, name="y_bf%d" % c, align_bytes=64)
+            if c in ROUND_ON_SCALAR:
+                nc.scalar.copy(woven(y_bf[:]), by_fours(y[:]))
+            else:
+                nc.vector.tensor_copy(woven(y_bf[:]), by_fours(y[:]))
+            y_codes = keep.tile([P, W], I32, name="y_codes%d" % c, align_bytes=64)
             nc.vector.quantize_mx(
                 out=y_codes[:].bitcast(FP8X4), scales=y_plane[:, lo:hi], in_=y_bf[:].rearrange("p c t -> p (c t)")
             )

@@ -20,11 +20,16 @@ PACK = 4
 LANES = 16
 W = 128
 CHUNKS = S // W
-Z_ON_VECTOR = (1, 3)
-H_ON_VECTOR = ()
+Z_ON_VECTOR = (0,)
+H_ON_VECTOR = (0,)
+WEAVE_ON_SCALAR = ()
+SIZE_TAGS = ["a","a","a2","a3"]
+EARLY = (0,)
+ORDER = [("z", 0), ("r", 0), ("z", 1), ("z", 2), ("z", 3), ("r", 1), ("r", 2), ("r", 3)]
 ROUND_ON_SCALAR = (1, 2)
-FETCH_ON_VECTOR = (0,)
-WARM = False
+FETCH_GROUPS = [(0,), (1, 2), (3,)]
+ROOT_GROUPS = [(0, 1), (2,), (3,)]
+FETCH_ON_VECTOR = ()
 
 
 def tile_picked_twpqgatebnorm_none_po_kernel(
@@ -101,7 +106,7 @@ def tile_picked_twpqgatebnorm_none_po_kernel(
             x_pick = keep.tile([P, S], U32, name=side + "_x_pick", tag="x_pick", align_bytes=64)
             nc.vector.tensor_copy(x_pick[:], x_tab[:].bitcast(U32).indirect(tokens_t[:]))
             d_codes = keep.tile([P, H], U32, name=side + "_d_codes", align_bytes=64)
-            nc.vector.tensor_copy(dealt(d_codes[:]), deal(d_pick[:]))
+            nc.vector.tensor_copy(dealt_words(d_codes[:]), deal_words(d_pick[:]))
             d_plane = keep.tile([P, H], U8, name=side + "_d_plane", align_bytes=64)
             nc.vector.tensor_copy(dealt(d_plane[:]), deal(placed[:, :H]))
             banks = []
@@ -119,6 +124,12 @@ def tile_picked_twpqgatebnorm_none_po_kernel(
                 )
                 banks.append(bank)
             return banks
+
+        def deal_words(src):
+            return src.rearrange("p (b i t) -> p b t i", i=4, t=PACK)
+
+        def dealt_words(dst):
+            return dst.rearrange("p (t b i) -> p b t i", i=4, t=PACK)
 
         w_codes = keep.tile([P, N], U32, name="w_codes", align_bytes=64)
         w_plane = reuse.tile([P, N], U8, name="w_plane", align_bytes=64, offset=4096 + 512)
@@ -148,7 +159,7 @@ def tile_picked_twpqgatebnorm_none_po_kernel(
             nc.scalar.activation(tile[:], a_banks[t][:], ACT.Copy, scale=gain[:, t : t + 1])
             half.append(tile)
 
-        nc.scalar.copy(dealt(w_codes[:]), deal(w_raw[:].bitcast(U32)))
+        nc.scalar.copy(dealt_words(w_codes[:]), deal_words(w_raw[:].bitcast(U32)))
 
         def woven(dst):
             return dst.rearrange("p (c i) t -> p c t i", i=4)
@@ -156,9 +167,15 @@ def tile_picked_twpqgatebnorm_none_po_kernel(
         def by_fours(src):
             return src.rearrange("p t (c i) -> p c t i", i=4)
 
+        early = {}
+        for c in EARLY:
+            early[c] = keep.tile([P, PACK, W], F32, name="other%d" % c)
         gated = keep.tile([P, PACK, S], F32, name="gated")
         for t in range(PACK):
             nc.vector.scalar_tensor_tensor(gated[:, t, :], gate[t][:], -2.0, half[t][:], ALU.mult, ALU.mult)
+            for c in EARLY:
+                lo, hi = W * c, W * (c + 1)
+                nc.vector.tensor_tensor(early[c][:, t, :], half[t][:].indirect(entries(n1_t, lo, hi)), gated[:, t, lo:hi], ALU.add)
 
         half_bias = keep.tile([P, 1], F32, name="half_bias")
         nc.gpsimd.memset(half_bias[:], 0.5)
@@ -166,20 +183,30 @@ def tile_picked_twpqgatebnorm_none_po_kernel(
         for t in range(PACK):
             inv.append(keep.tile([P, S], F32, name="inv%d" % t))
 
-        h_src = []
-        for c in range(CHUNKS):
+        h_src = {}
+        others = {}
+
+        def z_chunk(c):
             lo, hi = W * c, W * (c + 1)
-            other = keep.tile([P, PACK, W], F32, name="other%d" % c)
+            other = early[c] if c in EARLY else keep.tile([P, PACK, W], F32, name="other%d" % c)
             z_bf = keep.tile([P, W, PACK], BF16, name="z_bf%d" % c, align_bytes=64)
             if c in Z_ON_VECTOR:
-                for t in range(PACK):
+                for t in range(0 if c in EARLY else PACK):
                     nc.vector.tensor_tensor(other[:, t, :], half[t][:].indirect(entries(n1_t, lo, hi)), gated[:, t, lo:hi], ALU.add)
-                nc.vector.tensor_copy(woven(z_bf[:]), by_fours(other[:]))
+                if c in WEAVE_ON_SCALAR:
+                    nc.scalar.copy(woven(z_bf[:]), by_fours(other[:]))
+                else:
+                    nc.vector.tensor_copy(woven(z_bf[:]), by_fours(other[:]))
             else:
                 for t in range(PACK):
                     nc.scalar.activation(other[:, t, :], half[t][:].indirect(entries(n1_t, lo, hi)), ACT.Copy)
-                last_other = other
-                nc.vector.tensor_tensor(woven(z_bf[:]), by_fours(gated[:, :, lo:hi]), by_fours(other[:]), ALU.add)
+                others[c] = other
+                z_flat = keep.tile([P, PACK, W], BF16, name="z_flat%d" % c)
+                nc.vector.tensor_tensor(z_flat[:], gated[:, :, lo:hi], other[:], ALU.add)
+                if c in WEAVE_ON_SCALAR:
+                    nc.scalar.copy(woven(z_bf[:]), by_fours(z_flat[:]))
+                else:
+                    nc.vector.tensor_copy(woven(z_bf[:]), by_fours(z_flat[:]))
             z_codes = keep.tile([P, W], U32, name="z_codes%d" % c, align_bytes=64)
             z_plane = keep.tile([P, W], U8, name="z_plane%d" % c, align_bytes=64)
             nc.vector.quantize_mx(
@@ -197,14 +224,18 @@ def tile_picked_twpqgatebnorm_none_po_kernel(
                     start=True,
                     stop=True,
                 )
-            h_src.append(bank)
+            h_src[c] = bank
 
-        if WARM:
-            warm = keep.tile([P, 1], F32, name="warm")
-            nc.scalar.activation(warm[:], last_other[:, 3, 0:1], ACT.Abs_reciprocal_sqrt, bias=half_bias[:])
-        for c in range(CHUNKS):
-            lo, hi = W * c, W * (c + 1)
-            size = keep.tile([P, PACK, W], F32, name="size%d" % c)
+        roots = {}
+        for group in ROOT_GROUPS:
+            root = keep.tile([P, PACK, W * len(group)], F32, name="root%d" % group[0])
+            for c in group:
+                roots[c] = (root, group)
+
+        def root_chunk(c):
+            root, group = roots[c]
+            lo, hi = W * group[0], W * (group[-1] + 1)
+            size = keep.tile([P, PACK, W], F32, name="size%d" % c, tag=SIZE_TAGS[c])
             if c in H_ON_VECTOR:
                 h_sb = keep.tile([P, PACK, W], F32, name="h_sb%d" % c)
                 nc.vector.tensor_copy(h_sb[:], h_src[c][:])
@@ -212,28 +243,45 @@ def tile_picked_twpqgatebnorm_none_po_kernel(
                 h_src[c] = h_sb
             else:
                 nc.scalar.activation(size[:], h_src[c][:], ACT.Abs)
-            root = keep.tile([P, PACK, W], F32, name="root%d" % c)
-            nc.scalar.activation(root[:], size[:], ACT.Abs_reciprocal_sqrt, bias=half_bias[:])
-            for t in range(PACK):
-                nc.vector.tensor_tensor(inv[t][:, lo:hi], root[:, t, :], root[:, t, :], ALU.mult)
+            nc.scalar.activation(
+                root[:, :, W * c - lo : W * (c + 1) - lo], size[:], ACT.Abs_reciprocal_sqrt, bias=half_bias[:]
+            )
+            if c == group[-1]:
+                for t in range(PACK):
+                    nc.vector.tensor_tensor(inv[t][:, lo:hi], root[:, t, :], root[:, t, :], ALU.mult)
+
+        for kind, c in ORDER:
+            if kind == "z":
+                z_chunk(c)
+            elif kind == "w":
+                warm = keep.tile([P, 1], F32, name="warm")
+                nc.scalar.activation(warm[:], others[c][:, 3, 0:1], ACT.Abs_reciprocal_sqrt, bias=half_bias[:])
+            else:
+                root_chunk(c)
 
         out_rows = out_0.rearrange("(p t) j -> p t j", t=PACK)
         out_words = out_1[0].rearrange("p n t -> p (n t)").bitcast(I32)
         y_plane = keep.tile([P, S], U8, name="y_plane", align_bytes=64)
+        fetched = {}
+        for group in FETCH_GROUPS:
+            lo, hi = W * group[0], W * (group[-1] + 1)
+            tile = keep.tile([P, PACK, hi - lo], F32, name="fetched%d" % group[0])
+            for t in range(PACK):
+                if group[0] in H_ON_VECTOR:
+                    nc.vector.tensor_tensor(tile[:, t, :], inv[t][:].indirect(entries(n3_t, lo, hi)), h_src[group[0]][:, t, :], ALU.mult)
+                elif group[0] in FETCH_ON_VECTOR:
+                    nc.vector.tensor_copy(tile[:, t, :], inv[t][:].indirect(entries(n3_t, lo, hi)))
+                else:
+                    nc.scalar.activation(tile[:, t, :], inv[t][:].indirect(entries(n3_t, lo, hi)), ACT.Copy)
+            for c in group:
+                fetched[c] = tile[:, :, W * c - lo : W * (c + 1) - lo]
         for c in range(CHUNKS):
             lo, hi = W * c, W * (c + 1)
-            y = keep.tile([P, PACK, W], F32, name="y%d" % c)
             if c in H_ON_VECTOR:
-                for t in range(PACK):
-                    nc.vector.tensor_tensor(y[:, t, :], inv[t][:].indirect(entries(n3_t, lo, hi)), h_src[c][:, t, :], ALU.mult)
+                y = fetched[c]
             else:
-                fetched = keep.tile([P, PACK, W], F32, name="fetched%d" % c)
-                for t in range(PACK):
-                    if c in FETCH_ON_VECTOR:
-                        nc.vector.tensor_copy(fetched[:, t, :], inv[t][:].indirect(entries(n3_t, lo, hi)))
-                    else:
-                        nc.scalar.activation(fetched[:, t, :], inv[t][:].indirect(entries(n3_t, lo, hi)), ACT.Copy)
-                nc.vector.tensor_tensor(y[:], h_src[c][:], fetched[:], ALU.mult)
+                y = keep.tile([P, PACK, W], F32, name="y%d" % c)
+                nc.vector.tensor_tensor(y[:], h_src[c][:], fetched[c], ALU.mult)
             nc.sync.dma_start(out=out_rows[:, :, lo:hi], in_=y[:])
             y_bf = keep.tile([P, W, PACK], BF16, name="y_bf%d" % c, align_bytes=64)
             if c in ROUND_ON_SCALAR:

@@ -20,15 +20,17 @@ PACK = 4
 LANES = 16
 W = 128
 CHUNKS = S // W
-Z_ON_VECTOR = (0,)
-H_ON_VECTOR = (0,)
+Z_ON_VECTOR = (2,)
+H_ON_VECTOR = (0,1)
 WEAVE_ON_SCALAR = ()
-SIZE_TAGS = ["a","a","a2","a3"]
-EARLY = (0,)
-ORDER = [("z", 0), ("r", 0), ("z", 1), ("z", 2), ("z", 3), ("r", 1), ("r", 2), ("r", 3)]
-ROUND_ON_SCALAR = (1, 2)
-FETCH_GROUPS = [(0,), (1, 2), (3,)]
-ROOT_GROUPS = [(0, 1), (2,), (3,)]
+SIZE_TAGS = ["a","b","a","c"]
+EARLY = ()
+SQ_ON_SCALAR = ((3,2),(3,3))
+ROUND_GROUPS = [(0,1),(2,),(3,)]
+ORDER = [("z", 0), ("r", 0), ("z", 2), ("z", 1), ("r", 1), ("z", 3), ("r", 2), ("r", 3)]
+ROUND_ON_SCALAR = (0,2)
+FETCH_GROUPS = [(0,1),(2,3)]
+ROOT_GROUPS = [(0,),(1,),(2,),(3,)]
 FETCH_ON_VECTOR = ()
 
 
@@ -91,14 +93,14 @@ def tile_picked_twpqgatebnorm_none_po_kernel(
         def dealt(dst):
             return dst.rearrange("p (t m) -> p t m", t=PACK)
 
-        def coded_product(side, codes_t, tokens_t, picked_at, d_pick_at):
+        def coded_product(side, codes_t, tokens_t, picked_at, d_pick_at, queue):
             picked = reuse.tile([P, H + S], U8, name=side + "_picked", align_bytes=64, offset=picked_at)
             placed = keep.tile([P, H + S], U8, name=side + "_placed", align_bytes=64)
             nc.vector.memset(placed[:].bitcast(I32), 0)
             nc.vector.tensor_copy(picked[:, H:], x_rows[:].indirect(tokens_t[:]))
             nc.vector.tensor_copy(picked[:, :H], d_rows[:].indirect(codes_t[:]))
             for q in range(4):
-                nc.sync.dma_start(
+                queue.dma_start(
                     out=placed[32 * q : 32 * q + 4, :].bitcast(I32), in_=picked[32 * q : 32 * q + 32 : 8, :].bitcast(I32)
                 )
             d_pick = reuse.tile([P, H], U32, name=side + "_d_pick", align_bytes=64, offset=d_pick_at)
@@ -134,7 +136,7 @@ def tile_picked_twpqgatebnorm_none_po_kernel(
         w_codes = keep.tile([P, N], U32, name="w_codes", align_bytes=64)
         w_plane = reuse.tile([P, N], U8, name="w_plane", align_bytes=64, offset=4096 + 512)
 
-        b_banks = coded_product("b", k2_t, two_t, 4096, 8192)
+        b_banks = coded_product("b", k2_t, two_t, 4096, 8192, nc.sync)
         sig = []
         for t in range(PACK):
             tile = keep.tile([P, S], F32, name="sig%d" % t)
@@ -148,7 +150,7 @@ def tile_picked_twpqgatebnorm_none_po_kernel(
             for lo in (0, 256):
                 nc.scalar.activation(gate[t][:, lo : lo + 256], sig[t][:].indirect(entries(n2_t, lo, lo + 256)), ACT.Copy)
 
-        a_banks = coded_product("a", k1_t, offs_t, 4096 + 512, 4096 - 2048 + 256)
+        a_banks = coded_product("a", k1_t, offs_t, 4096 + 512, 4096 - 2048 + 256, nc.sync)
         for lo in (0, 256):
             nc.vector.tensor_copy(gate[3][:, lo : lo + 256], sig[3][:].indirect(entries(n2_t, lo, lo + 256)))
         nc.vector.tensor_copy(dealt(w_plane[:]), deal(w_rows[:]))
@@ -201,12 +203,7 @@ def tile_picked_twpqgatebnorm_none_po_kernel(
                 for t in range(PACK):
                     nc.scalar.activation(other[:, t, :], half[t][:].indirect(entries(n1_t, lo, hi)), ACT.Copy)
                 others[c] = other
-                z_flat = keep.tile([P, PACK, W], BF16, name="z_flat%d" % c)
-                nc.vector.tensor_tensor(z_flat[:], gated[:, :, lo:hi], other[:], ALU.add)
-                if c in WEAVE_ON_SCALAR:
-                    nc.scalar.copy(woven(z_bf[:]), by_fours(z_flat[:]))
-                else:
-                    nc.vector.tensor_copy(woven(z_bf[:]), by_fours(z_flat[:]))
+                nc.vector.tensor_tensor(woven(z_bf[:]), by_fours(gated[:, :, lo:hi]), by_fours(other[:]), ALU.add)
             z_codes = keep.tile([P, W], U32, name="z_codes%d" % c, align_bytes=64)
             z_plane = keep.tile([P, W], U8, name="z_plane%d" % c, align_bytes=64)
             nc.vector.quantize_mx(
@@ -226,6 +223,7 @@ def tile_picked_twpqgatebnorm_none_po_kernel(
                 )
             h_src[c] = bank
 
+        h_sb = keep.tile([P, PACK, W * len(H_ON_VECTOR)], F32, name="h_sb")
         roots = {}
         for group in ROOT_GROUPS:
             root = keep.tile([P, PACK, W * len(group)], F32, name="root%d" % group[0])
@@ -237,10 +235,9 @@ def tile_picked_twpqgatebnorm_none_po_kernel(
             lo, hi = W * group[0], W * (group[-1] + 1)
             size = keep.tile([P, PACK, W], F32, name="size%d" % c, tag=SIZE_TAGS[c])
             if c in H_ON_VECTOR:
-                h_sb = keep.tile([P, PACK, W], F32, name="h_sb%d" % c)
-                nc.vector.tensor_copy(h_sb[:], h_src[c][:])
-                nc.vector.scalar_tensor_tensor(size[:], h_sb[:], -1.0, h_sb[:], ALU.mult, ALU.max)
-                h_src[c] = h_sb
+                part = h_sb[:, :, W * (c - H_ON_VECTOR[0]) : W * (c - H_ON_VECTOR[0] + 1)]
+                nc.vector.tensor_copy(part, h_src[c][:])
+                nc.vector.scalar_tensor_tensor(size[:], part, -1.0, part, ALU.mult, ALU.max)
             else:
                 nc.scalar.activation(size[:], h_src[c][:], ACT.Abs)
             nc.scalar.activation(
@@ -248,7 +245,10 @@ def tile_picked_twpqgatebnorm_none_po_kernel(
             )
             if c == group[-1]:
                 for t in range(PACK):
-                    nc.vector.tensor_tensor(inv[t][:, lo:hi], root[:, t, :], root[:, t, :], ALU.mult)
+                    if (c, t) in SQ_ON_SCALAR:
+                        nc.scalar.activation(inv[t][:, lo:hi], root[:, t, :], ACT.Square)
+                    else:
+                        nc.vector.tensor_tensor(inv[t][:, lo:hi], root[:, t, :], root[:, t, :], ALU.mult)
 
         for kind, c in ORDER:
             if kind == "z":
@@ -262,37 +262,41 @@ def tile_picked_twpqgatebnorm_none_po_kernel(
         out_rows = out_0.rearrange("(p t) j -> p t j", t=PACK)
         out_words = out_1[0].rearrange("p n t -> p (n t)").bitcast(I32)
         y_plane = keep.tile([P, S], U8, name="y_plane", align_bytes=64)
-        fetched = {}
+        y_of = {}
+        codes_of = {}
         for group in FETCH_GROUPS:
             lo, hi = W * group[0], W * (group[-1] + 1)
-            tile = keep.tile([P, PACK, hi - lo], F32, name="fetched%d" % group[0])
-            for t in range(PACK):
-                if group[0] in H_ON_VECTOR:
-                    nc.vector.tensor_tensor(tile[:, t, :], inv[t][:].indirect(entries(n3_t, lo, hi)), h_src[group[0]][:, t, :], ALU.mult)
-                elif group[0] in FETCH_ON_VECTOR:
-                    nc.vector.tensor_copy(tile[:, t, :], inv[t][:].indirect(entries(n3_t, lo, hi)))
-                else:
-                    nc.scalar.activation(tile[:, t, :], inv[t][:].indirect(entries(n3_t, lo, hi)), ACT.Copy)
+            y = keep.tile([P, PACK, hi - lo], F32, name="y%d" % group[0])
+            if group[0] in H_ON_VECTOR:
+                for t in range(PACK):
+                    nc.vector.tensor_tensor(y[:, t, :], inv[t][:].indirect(entries(n3_t, lo, hi)), h_sb[:, t, :], ALU.mult)
+                    nc.sync.dma_start(out=out_rows[:, t, lo:hi], in_=y[:, t, :])
+            else:
+                fetched = keep.tile([P, PACK, hi - lo], F32, name="fetched%d" % group[0])
+                for t in range(PACK):
+                    nc.scalar.activation(fetched[:, t, :], inv[t][:].indirect(entries(n3_t, lo, hi)), ACT.Copy)
+                for c in group:
+                    part = slice(W * c - lo, W * (c + 1) - lo)
+                    nc.vector.tensor_tensor(y[:, :, part], h_src[c][:], fetched[:, :, part], ALU.mult)
+                    nc.sync.dma_start(out=out_rows[:, :, W * c : W * (c + 1)], in_=y[:, :, part])
+            codes_of[lo] = keep.tile([P, hi - lo], I32, name="y_codes%d" % group[0], align_bytes=64)
             for c in group:
-                fetched[c] = tile[:, :, W * c - lo : W * (c + 1) - lo]
-        for c in range(CHUNKS):
-            lo, hi = W * c, W * (c + 1)
-            if c in H_ON_VECTOR:
-                y = fetched[c]
+                y_of[c] = (y, lo)
+        for group in ROUND_GROUPS:
+            lo, hi = W * group[0], W * (group[-1] + 1)
+            tile, first = y_of[group[0]]
+            y = tile[:, :, lo - first : hi - first]
+            y_bf = keep.tile([P, hi - lo, PACK], BF16, name="y_bf%d" % group[0], align_bytes=64)
+            if group[0] in ROUND_ON_SCALAR:
+                nc.scalar.copy(woven(y_bf[:]), by_fours(y))
             else:
-                y = keep.tile([P, PACK, W], F32, name="y%d" % c)
-                nc.vector.tensor_tensor(y[:], h_src[c][:], fetched[c], ALU.mult)
-            nc.sync.dma_start(out=out_rows[:, :, lo:hi], in_=y[:])
-            y_bf = keep.tile([P, W, PACK], BF16, name="y_bf%d" % c, align_bytes=64)
-            if c in ROUND_ON_SCALAR:
-                nc.scalar.copy(woven(y_bf[:]), by_fours(y[:]))
-            else:
-                nc.vector.tensor_copy(woven(y_bf[:]), by_fours(y[:]))
-            y_codes = keep.tile([P, W], I32, name="y_codes%d" % c, align_bytes=64)
+                nc.vector.tensor_copy(woven(y_bf[:]), by_fours(y))
+            y_codes = codes_of[first]
             nc.vector.quantize_mx(
-                out=y_codes[:].bitcast(FP8X4), scales=y_plane[:, lo:hi], in_=y_bf[:].rearrange("p c t -> p (c t)")
+                out=y_codes[:, lo - first : hi - first].bitcast(FP8X4), scales=y_plane[:, lo:hi], in_=y_bf[:].rearrange("p c t -> p (c t)")
             )
-            nc.sync.dma_start(out=out_words[:, lo:hi], in_=y_codes[:])
+            if hi == first + 2 * W:
+                nc.sync.dma_start(out=out_words[:, first:hi], in_=y_codes[:])
         for q in range(4):
             queue = nc.sync if q % 2 == 0 else nc.scalar
             queue.dma_start(

from contextlib import ExitStack

import concourse.mybir as mybir

K, T, S, N, G, H = 512, 1024, 512, 512, 2048, 512
FLOPS = 2 * K * H * S * 2 + 2 * H * N * S

F32 = mybir.dt.float32
BF16 = mybir.dt.bfloat16
I32 = mybir.dt.int32
U32 = mybir.dt.uint32
U16 = mybir.dt.uint16
U8 = mybir.dt.uint8
FP8X4 = mybir.dt.float8_e4m3fn_x4
ACT = mybir.ActivationFunctionType
ALU = mybir.AluOpType

P = 128
PACK = 4
LANES = 16
W = 128
CHUNKS = S // W
Z_ON_VECTOR = (2,)
H_ON_VECTOR = (0,1)
WEAVE_ON_SCALAR = ()
SIZE_TAGS = ["a","b","a","c"]
EARLY = ()
SQ_ON_SCALAR = ((3,2),(3,3))
ROUND_GROUPS = [(0,1),(2,),(3,)]
ORDER = [("z", 0), ("r", 0), ("z", 2), ("z", 1), ("r", 1), ("z", 3), ("r", 2), ("r", 3)]
ROUND_ON_SCALAR = (0,2)
FETCH_GROUPS = [(0,1),(2,3)]
ROOT_GROUPS = [(0,),(1,),(2,),(3,)]
FETCH_ON_VECTOR = ()


def tile_picked_twpqgatebnorm_none_po_kernel(
    tc, x_words, x_scales, d_words, d_scales, gn, w1_words, w1_scales, offs, k1, two, k2, n1, n2, n3, out_0, out_1, out_2
):
    nc = tc.nc

    with ExitStack() as ctx:
        keep = ctx.enter_context(tc.tile_pool(name="keep", bufs=1))
        reuse = ctx.enter_context(tc.tile_pool(name="reuse", bufs=1))
        psum = ctx.enter_context(tc.psum_pool(name="psum", bufs=1))

        def load_list(name, src):
            tile = keep.tile([P, S // LANES], U16, name=name)
            nc.sync.dma_start(tile[:], src)
            return tile

        def entries(lst, lo, hi):
            return lst[:, lo // LANES : hi // LANES]

        def load_words(name, src, cols, queue):
            tile = keep.tile([P, cols], I32, name=name, align_bytes=64)
            queue.dma_start(out=tile[:], in_=src[0].rearrange("p n t -> p (n t)").bitcast(I32))
            return tile

        def load_scale_rows(name, src, cols):
            tile = keep.tile([P, cols], U8, name=name, align_bytes=64)
            rows = src[0].bitcast(I32)
            nc.sync.dma_start(out=tile[:].bitcast(I32), in_=rows.unsqueeze(1).broadcast_to([16, 8, cols // 4]))
            return tile

        two_t = load_list("two_t", two)
        x_rows = load_scale_rows("x_rows", x_scales, T)
        k2_t = load_list("k2_t", k2)
        d_rows = load_scale_rows("d_rows", d_scales, G)
        d_tab = load_words("d_tab", d_words, G, nc.sync)
        n2_t = load_list("n2_t", n2)
        n1_t = load_list("n1_t", n1)
        n3_t = load_list("n3_t", n3)
        x_tab = load_words("x_tab", x_words, T, nc.sync)
        k1_t = load_list("k1_t", k1)
        offs_t = load_list("offs_t", offs)
        w_raw = load_words("w_raw", w1_words, N, nc.sync)

        gn_t = keep.tile([P, PACK], F32, name="gn_t")
        nc.gpsimd.dma_start(out=gn_t[:], in_=gn.rearrange("(p t) o -> p (t o)", t=PACK))
        w_rows = keep.tile([P, N], U8, name="w_rows", align_bytes=64)
        nc.gpsimd.memset(w_rows[:].bitcast(I32), 0)
        for q in range(4):
            nc.gpsimd.dma_start(
                out=w_rows[32 * q : 32 * q + 4, :].bitcast(I32), in_=w1_scales[0, 4 * q : 4 * q + 4, :].bitcast(I32)
            )
        gain = keep.tile([P, PACK], F32, name="gain")
        nc.gpsimd.tensor_scalar(gain[:], gn_t[:], -0.5 * 0.0625, 0.0, ALU.mult, ALU.add)

        def deal(src):
            return src.rearrange("p (m t) -> p t m", t=PACK)

        def dealt(dst):
            return dst.rearrange("p (t m) -> p t m", t=PACK)

        def coded_product(side, codes_t, tokens_t, picked_at, d_pick_at, queue):
            picked = reuse.tile([P, H + S], U8, name=side + "_picked", align_bytes=64, offset=picked_at)
            placed = keep.tile([P, H + S], U8, name=side + "_placed", align_bytes=64)
            nc.vector.memset(placed[:].bitcast(I32), 0)
            nc.vector.tensor_copy(picked[:, H:], x_rows[:].indirect(tokens_t[:]))
            nc.vector.tensor_copy(picked[:, :H], d_rows[:].indirect(codes_t[:]))
            for q in range(4):
                queue.dma_start(
                    out=placed[32 * q : 32 * q + 4, :].bitcast(I32), in_=picked[32 * q : 32 * q + 32 : 8, :].bitcast(I32)
                )
            d_pick = reuse.tile([P, H], U32, name=side + "_d_pick", align_bytes=64, offset=d_pick_at)
            nc.vector.tensor_copy(d_pick[:], d_tab[:].bitcast(U32).indirect(codes_t[:]))
            x_pick = keep.tile([P, S], U32, name=side + "_x_pick", tag="x_pick", align_bytes=64)
            nc.vector.tensor_copy(x_pick[:], x_tab[:].bitcast(U32).indirect(tokens_t[:]))
            d_codes = keep.tile([P, H], U32, name=side + "_d_codes", align_bytes=64)
            nc.vector.tensor_copy(dealt_words(d_codes[:]), deal_words(d_pick[:]))
            d_plane = keep.tile([P, H], U8, name=side + "_d_plane", align_bytes=64)
            nc.vector.tensor_copy(dealt(d_plane[:]), deal(placed[:, :H]))
            banks = []
            for t in range(PACK):
                bank = psum.tile([P, S], F32, name=side + "_bank%d" % t, tag=side + "_bank%d" % t)
                cols = slice(P * t, P * (t + 1))
                nc.tensor.matmul_mx(
                    out=bank[:],
                    lhsT=d_codes[:, cols].bitcast(FP8X4),
                    lhsT_scale=d_plane[:, cols],
                    rhs=x_pick[:].bitcast(FP8X4),
                    rhs_scale=placed[:, H:],
                    start=True,
                    stop=True,
                )
                banks.append(bank)
            return banks

        def deal_words(src):
            return src.rearrange("p (b i t) -> p b t i", i=4, t=PACK)

        def dealt_words(dst):
            return dst.rearrange("p (t b i) -> p b t i", i=4, t=PACK)

        w_codes = keep.tile([P, N], U32, name="w_codes", align_bytes=64)
        w_plane = reuse.tile([P, N], U8, name="w_plane", align_bytes=64, offset=4096 + 512)

        b_banks = coded_product("b", k2_t, two_t, 4096, 8192, nc.sync)
        sig = []
        for t in range(PACK):
            tile = keep.tile([P, S], F32, name="sig%d" % t)
            nc.scalar.activation(tile[:], b_banks[t][:], ACT.Sigmoid, scale=0.0625)
            sig.append(tile)
        gate = []
        for t in range(PACK - 1):
            gate.append(keep.tile([P, S], F32, name="gate%d" % t))
        gate.append(reuse.tile([P, S], F32, name="gate3", align_bytes=64, offset=4096 + 512 + 768))
        for t in range(PACK - 1):
            for lo in (0, 256):
                nc.scalar.activation(gate[t][:, lo : lo + 256], sig[t][:].indirect(entries(n2_t, lo, lo + 256)), ACT.Copy)

        a_banks = coded_product("a", k1_t, offs_t, 4096 + 512, 4096 - 2048 + 256, nc.sync)
        for lo in (0, 256):
            nc.vector.tensor_copy(gate[3][:, lo : lo + 256], sig[3][:].indirect(entries(n2_t, lo, lo + 256)))
        nc.vector.tensor_copy(dealt(w_plane[:]), deal(w_rows[:]))

        half = []
        for t in range(PACK):
            tile = keep.tile([P, S], F32, name="half%d" % t)
            nc.scalar.activation(tile[:], a_banks[t][:], ACT.Copy, scale=gain[:, t : t + 1])
            half.append(tile)

        nc.scalar.copy(dealt_words(w_codes[:]), deal_words(w_raw[:].bitcast(U32)))

        def woven(dst):
            return dst.rearrange("p (c i) t -> p c t i", i=4)

        def by_fours(src):
            return src.rearrange("p t (c i) -> p c t i", i=4)

        early = {}
        for c in EARLY:
            early[c] = keep.tile([P, PACK, W], F32, name="other%d" % c)
        gated = keep.tile([P, PACK, S], F32, name="gated")
        for t in range(PACK):
            nc.vector.scalar_tensor_tensor(gated[:, t, :], gate[t][:], -2.0, half[t][:], ALU.mult, ALU.mult)
            for c in EARLY:
                lo, hi = W * c, W * (c + 1)
                nc.vector.tensor_tensor(early[c][:, t, :], half[t][:].indirect(entries(n1_t, lo, hi)), gated[:, t, lo:hi], ALU.add)

        half_bias = keep.tile([P, 1], F32, name="half_bias")
        nc.gpsimd.memset(half_bias[:], 0.5)
        inv = []
        for t in range(PACK):
            inv.append(keep.tile([P, S], F32, name="inv%d" % t))

        h_src = {}
        others = {}

        def z_chunk(c):
            lo, hi = W * c, W * (c + 1)
            other = early[c] if c in EARLY else keep.tile([P, PACK, W], F32, name="other%d" % c)
            z_bf = keep.tile([P, W, PACK], BF16, name="z_bf%d" % c, align_bytes=64)
            if c in Z_ON_VECTOR:
                for t in range(0 if c in EARLY else PACK):
                    nc.vector.tensor_tensor(other[:, t, :], half[t][:].indirect(entries(n1_t, lo, hi)), gated[:, t, lo:hi], ALU.add)
                if c in WEAVE_ON_SCALAR:
                    nc.scalar.copy(woven(z_bf[:]), by_fours(other[:]))
                else:
                    nc.vector.tensor_copy(woven(z_bf[:]), by_fours(other[:]))
            else:
                for t in range(PACK):
                    nc.scalar.activation(other[:, t, :], half[t][:].indirect(entries(n1_t, lo, hi)), ACT.Copy)
                others[c] = other
                nc.vector.tensor_tensor(woven(z_bf[:]), by_fours(gated[:, :, lo:hi]), by_fours(other[:]), ALU.add)
            z_codes = keep.tile([P, W], U32, name="z_codes%d" % c, align_bytes=64)
            z_plane = keep.tile([P, W], U8, name="z_plane%d" % c, align_bytes=64)
            nc.vector.quantize_mx(
                out=z_codes[:].bitcast(FP8X4), scales=z_plane[:], in_=z_bf[:].rearrange("p c t -> p (c t)")
            )
            bank = psum.tile([P, PACK, W], F32, name="h_bank%d" % c, tag="b_bank%d" % c)
            for t in range(PACK):
                cols = slice(P * t, P * (t + 1))
                nc.tensor.matmul_mx(
                    out=bank[:, t, :],
                    lhsT=w_codes[:, cols].bitcast(FP8X4),
                    lhsT_scale=w_plane[:, cols],
                    rhs=z_codes[:].bitcast(FP8X4),
                    rhs_scale=z_plane[:],
                    start=True,
                    stop=True,
                )
            h_src[c] = bank

        h_sb = keep.tile([P, PACK, W * len(H_ON_VECTOR)], F32, name="h_sb")
        roots = {}
        for group in ROOT_GROUPS:
            root = keep.tile([P, PACK, W * len(group)], F32, name="root%d" % group[0])
            for c in group:
                roots[c] = (root, group)

        def root_chunk(c):
            root, group = roots[c]
            lo, hi = W * group[0], W * (group[-1] + 1)
            size = keep.tile([P, PACK, W], F32, name="size%d" % c, tag=SIZE_TAGS[c])
            if c in H_ON_VECTOR:
                part = h_sb[:, :, W * (c - H_ON_VECTOR[0]) : W * (c - H_ON_VECTOR[0] + 1)]
                nc.vector.tensor_copy(part, h_src[c][:])
                nc.vector.scalar_tensor_tensor(size[:], part, -1.0, part, ALU.mult, ALU.max)
            else:
                nc.scalar.activation(size[:], h_src[c][:], ACT.Abs)
            nc.scalar.activation(
                root[:, :, W * c - lo : W * (c + 1) - lo], size[:], ACT.Abs_reciprocal_sqrt, bias=half_bias[:]
            )
            if c == group[-1]:
                for t in range(PACK):
                    if (c, t) in SQ_ON_SCALAR:
                        nc.scalar.activation(inv[t][:, lo:hi], root[:, t, :], ACT.Square)
                    else:
                        nc.vector.tensor_tensor(inv[t][:, lo:hi], root[:, t, :], root[:, t, :], ALU.mult)

        for kind, c in ORDER:
            if kind == "z":
                z_chunk(c)
            elif kind == "w":
                warm = keep.tile([P, 1], F32, name="warm")
                nc.scalar.activation(warm[:], others[c][:, 3, 0:1], ACT.Abs_reciprocal_sqrt, bias=half_bias[:])
            else:
                root_chunk(c)

        out_rows = out_0.rearrange("(p t) j -> p t j", t=PACK)
        out_words = out_1[0].rearrange("p n t -> p (n t)").bitcast(I32)
        y_plane = keep.tile([P, S], U8, name="y_plane", align_bytes=64)
        y_of = {}
        codes_of = {}
        for group in FETCH_GROUPS:
            lo, hi = W * group[0], W * (group[-1] + 1)
            y = keep.tile([P, PACK, hi - lo], F32, name="y%d" % group[0])
            if group[0] in H_ON_VECTOR:
                for t in range(PACK):
                    nc.vector.tensor_tensor(y[:, t, :], inv[t][:].indirect(entries(n3_t, lo, hi)), h_sb[:, t, :], ALU.mult)
                    nc.sync.dma_start(out=out_rows[:, t, lo:hi], in_=y[:, t, :])
            else:
                fetched = keep.tile([P, PACK, hi - lo], F32, name="fetched%d" % group[0])
                for t in range(PACK):
                    nc.scalar.activation(fetched[:, t, :], inv[t][:].indirect(entries(n3_t, lo, hi)), ACT.Copy)
                for c in group:
                    part = slice(W * c - lo, W * (c + 1) - lo)
                    nc.vector.tensor_tensor(y[:, :, part], h_src[c][:], fetched[:, :, part], ALU.mult)
                    nc.sync.dma_start(out=out_rows[:, :, W * c : W * (c + 1)], in_=y[:, :, part])
            codes_of[lo] = keep.tile([P, hi - lo], I32, name="y_codes%d" % group[0], align_bytes=64)
            for c in group:
                y_of[c] = (y, lo)
        for group in ROUND_GROUPS:
            lo, hi = W * group[0], W * (group[-1] + 1)
            tile, first = y_of[group[0]]
            y = tile[:, :, lo - first : hi - first]
            y_bf = keep.tile([P, hi - lo, PACK], BF16, name="y_bf%d" % group[0], align_bytes=64)
            if group[0] in ROUND_ON_SCALAR:
                nc.scalar.copy(woven(y_bf[:]), by_fours(y))
            else:
                nc.vector.tensor_copy(woven(y_bf[:]), by_fours(y))
            y_codes = codes_of[first]
            nc.vector.quantize_mx(
                out=y_codes[:, lo - first : hi - first].bitcast(FP8X4), scales=y_plane[:, lo:hi], in_=y_bf[:].rearrange("p c t -> p (c t)")
            )
            if hi == first + 2 * W:
                nc.sync.dma_start(out=out_words[:, first:hi], in_=y_codes[:])
        for q in range(4):
            queue = nc.sync if q % 2 == 0 else nc.scalar
            queue.dma_start(
                out=out_2[0, 4 * q : 4 * q + 4, :].bitcast(I32), in_=y_plane[32 * q : 32 * q + 4, :].bitcast(I32)
            )
